import numpy as np
import ml_dtypes


def mxq(x, axis, fmt="e4m3"):
    dtype, down = {"e4m3": (ml_dtypes.float8_e4m3fn, 7), "e5m2": (ml_dtypes.float8_e5m2, 14)}[fmt]
    v = np.moveaxis(np.asarray(x, np.float32).astype(ml_dtypes.bfloat16).astype(np.float64), axis, -1)
    blocks = v.reshape(v.shape[:-1] + (-1, 32))
    amax = np.abs(blocks).max(-1, keepdims=True)
    byte = np.maximum(np.where(amax > 0, np.frexp(amax)[1] - 1 + 127, 0) - down, 1)
    scale = np.exp2(byte - 127.0)
    codes = (blocks / scale).astype(np.float32).astype(dtype).astype(np.float64)
    return np.moveaxis((codes * scale).reshape(v.shape), -1, axis)


WIDE = False


def mx_kscale(k):
    if not WIDE:
        return np.ones(k)
    levels = np.array([10, -10, 5, -5, 0])
    if k % 512:
        return np.exp2(np.random.permutation(np.resize(levels, k // 32))).repeat(32)
    a = np.empty((k // 512, 16))
    for p in range(k // 512):
        a[p, :8] = np.random.permutation(np.resize(levels, 8))
        for g in range(8):
            far = levels[np.abs(levels - a[p, g]) >= 10]
            a[p, g + 8] = far[np.random.randint(len(far))]
    return np.exp2(a.ravel()).repeat(32)


def f64(x):
    return np.asarray(x).astype(np.float64)


def striped(idx):
    return np.tile(idx.reshape(-1, 16).T, (8, 1)).astype(np.uint16)


def unstriped(offs):
    return offs[:16].T.reshape(-1).astype(np.int64)


E2M1 = np.array([0.0, 0.5, 1.0, 1.5, 2.0, 3.0, 4.0, 6.0, -0.0, -0.5, -1.0, -1.5, -2.0, -3.0, -4.0, -6.0])


def pack_weight(w, fmt):
    k, n = w.shape
    w = f64(np.asarray(w, np.float32).astype(ml_dtypes.bfloat16)).reshape(k // 32, 32, n)
    amax = np.abs(w).max(1)
    if fmt == "e4m3":
        byte = np.frexp(amax)[1] - 1 + 127 - 7
    else:
        mant, ex = np.frexp(amax / 6.0)
        byte = np.where(mant > 0.5, ex, ex - 1) + 127
    byte = np.clip(np.where(amax > 0, byte, 1), 1, 254)
    scaled = (w * np.exp2(127.0 - byte)[:, None, :]).reshape(k, n).astype(np.float32)
    by_word = np.ascontiguousarray(scaled.reshape(k // 512, 128, 4, n).transpose(0, 1, 3, 2))
    if fmt == "e4m3":
        words = by_word.astype(ml_dtypes.float8_e4m3fn).view(np.uint8)
    else:
        c = by_word.astype(ml_dtypes.float4_e2m1fn).view(np.uint8) & 0xF
        words = (c[..., 0::2] | (c[..., 1::2] << 4)).reshape(k // 512, 128, 2 * n)
    return np.ascontiguousarray(words), np.ascontiguousarray(byte.astype(np.uint8).reshape(k // 512, 16, n))


def unpack_weight(words, scales, fmt):
    g, _, n = scales.shape
    words = np.ascontiguousarray(words).reshape(g, 128, n, -1)
    if fmt == "e4m3":
        vals = words.view(ml_dtypes.float8_e4m3fn).astype(np.float64)
    else:
        nib = np.empty((g, 128, n, 4), np.uint8)
        nib[..., 0::2] = words & 0xF
        nib[..., 1::2] = words >> 4
        vals = E2M1[nib]
    vals = vals * np.repeat(np.exp2(scales.astype(np.float64) - 127.0), 8, axis=1)[..., None]
    return vals.transpose(0, 1, 3, 2).reshape(g * 512, n)


def gelu(v):
    return 0.5 * v * (1.0 + np.tanh(np.sqrt(2.0 / np.pi) * (v + 0.044715 * v**3)))


K, T, H, S, T3, S2 = 1536, 2048, 1024, 512, 2048, 512

def setup_inputs():
    n = np.random.standard_normal
    s = mx_kscale(K)[:, None]
    u = mx_kscale(H)[:, None]
    tab_words, tab_scales = pack_weight(n((K, T)) * s, "e4m3")
    tab2_words, tab2_scales = pack_weight(n((H, T3)) / np.sqrt(H) / u, "e4m3")
    tab3_words, tab3_scales = pack_weight(n((H, T3)) / np.sqrt(H) / u, "e4m3")
    w4_words, w4_scales = pack_weight(0.8 * n((K, H)) / np.sqrt(K) / s * u.T, "e2m1")
    return {
        "tab_words": tab_words, "tab_scales": tab_scales,
        "offs": striped(np.random.permutation(T)[:S]),
        "tab2_words": tab2_words, "tab2_scales": tab2_scales,
        "offs2": striped(np.random.permutation(T3)[:S2]),
        "tab3_words": tab3_words, "tab3_scales": tab3_scales,
        "offs3": striped(np.random.permutation(T3)[:S2]),
        "w1": (1.2 * n((K, H)) / np.sqrt(K) / s).astype(np.float32),
        "b1": (0.6 * n(H)).astype(np.float32),
        "gain": (1.4 * np.exp(0.3 * n(H)) * u[:, 0]).astype(np.float32),
        "w4_words": w4_words, "w4_scales": w4_scales,
        "res": (0.7 * n((H, S)) * u).astype(np.float32),
        "fit": np.exp(0.4 * n((S2, S))).astype(np.float32),
    }

def reference(tab_words, tab_scales, offs, tab2_words, tab2_scales, offs2,
              tab3_words, tab3_scales, offs3, w1, b1, gain, w4_words, w4_scales, res, fit):
    v = unpack_weight(tab_words, tab_scales, "e4m3")[:, unstriped(offs)]
    v2 = unpack_weight(tab2_words, tab2_scales, "e4m3")[:, unstriped(offs2)]
    v3 = unpack_weight(tab3_words, tab3_scales, "e4m3")[:, unstriped(offs3)]
    w4 = unpack_weight(w4_words, w4_scales, "e2m1")
    hd = f64(gain)[:, None] * np.tanh((mxq(f64(w1), 0, "e4m3").T @ v) + f64(b1)[:, None])
    ht = (w4.T @ v) + f64(res)
    e2 = v2.T @ mxq(hd, 0, "e4m3")
    e3 = v3.T @ mxq(ht, 0, "e4m3")
    return np.maximum(f64(fit) * e2, e3)

from contextlib import ExitStack

import concourse.mybir as mybir

K, T, H, S = 1536, 2048, 1024, 512
FLOPS = 2 * (2 * K * H * S + 2 * H * S * S)

F32 = mybir.dt.float32
BF16 = mybir.dt.bfloat16
I32 = mybir.dt.int32
U32 = mybir.dt.uint32
U16 = mybir.dt.uint16
U8 = mybir.dt.uint8
FP8X4 = mybir.dt.float8_e4m3fn_x4
FP4X4 = mybir.dt.float4_e2m1fn_x4
ALU = mybir.AluOpType
ACT = mybir.ActivationFunctionType

P = 128
PACK = 4
PASS = P * PACK
KP = K // PASS
HP = H // PASS
MT = S // P


def tile_list_donor_team_scores_kernel(
    tc, tab_words, tab_scales, offs, tab2_words, tab2_scales, offs2, tab3_words, tab3_scales, offs3,
    w1, b1, gain, w4_words, w4_scales, res, fit, out,
):
    nc = tc.nc
    with ExitStack() as ctx:
        keep = ctx.enter_context(tc.tile_pool(name="keep", bufs=1))
        ring = ctx.enter_context(tc.tile_pool(name="ring", bufs=2))
        psum = ctx.enter_context(tc.psum_pool(name="psum", bufs=8))

        def held(name, shape, dtype):
            return keep.tile(shape, dtype, name=name, align_bytes=64)

        lists = [held("list%d" % i, [P, S // 16], U16) for i in range(3)]
        w4_raw = held("w4_raw", [P, KP * H], U16)
        w4_dealt = held("w4_dealt", [P, KP * H], U16)
        w4_sc_raw = held("w4_sc_raw", [P, KP * H], U8)
        w4_sc = held("w4_sc", [P, KP * H], U8)
        v_sc_all = held("v_sc_all", [P, KP * T], U8)
        v2_sc_all = held("v2_sc_all", [P, T], U8)
        v3_sc_all = held("v3_sc_all", [P, T], U8)
        bias = held("bias", [P, HP, PACK], F32)
        gains = held("gains", [P, HP, PACK], F32)

        def load_side_by_side(tile, scales):
            rows = scales.bitcast(I32).rearrange("a (q r) n -> r q a n", r=4)
            view = tile[:].bitcast(I32).rearrange("p (a n) -> p a n", a=KP)
            for r in range(4):
                nc.sync.dma_start(out=view[r:P:32], in_=rows[r])

        def load_stacked(tile, scales):
            rows = scales.bitcast(I32)
            for q in range(4):
                nc.gpsimd.dma_start(out=tile[32 * q : 32 * q + 4 * HP, :].bitcast(I32), in_=rows[:, 4 * q : 4 * q + 4, :])

        def load_words(name, words, a):
            tile = held("%s_all%d" % (name, a), [P, T], U32)
            nc.sync.dma_start(out=tile[:].bitcast(I32), in_=words[a].rearrange("p t i -> p (t i)").bitcast(I32))
            return tile

        def load_w1(b, a):
            tile = ring.tile([P, PACK, PASS], F32, name="w1_raw", bufs=5)
            rows = w1[a * PASS : (a + 1) * PASS, b * PASS : (b + 1) * PASS]
            nc.sync.dma_start(out=tile[:], in_=rows.rearrange("(p j) c -> p j c", j=PACK))
            return tile

        def load_res(b):
            tile = held("res%d" % b, [P, PACK, S], F32)
            nc.sync.dma_start(out=tile[:], in_=res[b * PASS : (b + 1) * PASS, :].rearrange("(p t) j -> p t j", t=PACK))
            return tile

        def gather(name, window, offsets, dtype, pieces=1):
            tile = held(name, [P, S], dtype)
            n = S // pieces
            for i in range(pieces):
                nc.vector.tensor_copy(
                    out=tile[:, i * n : (i + 1) * n], in_=window.indirect(offsets[:, i * n // 16 : (i + 1) * n // 16])
                )
            return tile

        def quantize(name, grouped):
            codes = held(name + "_codes", [P, PASS], U32)
            scales = held(name + "_scales", [P, PASS], U8)
            nc.vector.quantize_mx(out=codes[:].bitcast(FP8X4), scales=scales[:], in_=grouped[:].rearrange("p c t -> p (c t)"))
            return codes, scales

        def quantize_w1(b, a, raw):
            grouped = ring.tile([P, PASS, PACK], BF16, name="w1_grouped", bufs=3, align_bytes=64)
            nc.scalar.copy(out=grouped[:].rearrange("p (t m) j -> p m j t", t=PACK), in_=raw[:].rearrange("p j (m t) -> p m j t", t=PACK))
            return quantize("w1_%d_%d" % (b, a), grouped)

        def donor_features(b, w1q, v, v_sc):
            th = ring.tile([P, PACK, S], F32, name="th")
            for t in range(PACK):
                acc = psum.tile([P, S], F32, name="acc")
                cols = slice(t * P, (t + 1) * P)
                for a in range(KP):
                    nc.tensor.matmul_mx(
                        out=acc[:], lhsT=w1q[a][0][:, cols].bitcast(FP8X4), lhsT_scale=w1q[a][1][:, cols],
                        rhs=v[a][:].bitcast(FP8X4), rhs_scale=v_sc[a][:], start=(a == 0), stop=(a == KP - 1),
                    )
                nc.scalar.activation(out=th[:, t, :], in_=acc[:], func=ACT.Tanh, bias=bias[:, b, t : t + 1])
            grouped = ring.tile([P, S, PACK], BF16, name="hd_grouped", align_bytes=64)
            nc.vector.tensor_tensor(
                out=grouped[:].rearrange("p (c i) t -> p c t i", i=4),
                in0=th[:].rearrange("p t (c i) -> p c t i", i=4),
                in1=gains[:, b, :].unsqueeze(1).unsqueeze(3).to_broadcast([P, S // 4, PACK, 4]),
                op=ALU.mult,
            )
            return quantize("hd%d" % b, grouped)

        def team_features(b, res_b, v, v_sc):
            grouped = ring.tile([P, S, PACK], BF16, name="ht_grouped", align_bytes=64)
            for jb in range(MT):
                js = slice(jb * P, (jb + 1) * P)
                acc = psum.tile([P, S], F32, name="acc")
                for t in range(PACK):
                    for a in range(KP):
                        c0 = a * H + b * PASS + t * P
                        nc.tensor.matmul_mx(
                            out=acc[:, t * P : (t + 1) * P], lhsT=w4_dealt[:, c0 : c0 + P].bitcast(FP4X4),
                            lhsT_scale=w4_sc[:, c0 : c0 + P],
                            rhs=v[a][:, js].bitcast(FP8X4), rhs_scale=v_sc[a][:, js], start=(a == 0), stop=(a == KP - 1),
                        )
                nc.vector.tensor_tensor(
                    out=grouped[:, js, :].rearrange("p (c i) t -> p c t i", i=4),
                    in0=acc[:].rearrange("p (t c i) -> p c t i", t=PACK, i=4),
                    in1=res_b[:, :, js].rearrange("p t (c i) -> p c t i", i=4),
                    op=ALU.add,
                )
            return quantize("ht%d" % b, grouped)

        def scores(m, words, planes, features):
            acc = psum.tile([P, S], F32, name="acc")
            cols = slice(m * P, (m + 1) * P)
            for b in range(HP):
                nc.tensor.matmul_mx(
                    out=acc[:], lhsT=words[b][:, cols].bitcast(FP8X4), lhsT_scale=planes[4 * b :, cols],
                    rhs=features[b][0][:].bitcast(FP8X4), rhs_scale=features[b][1][:], start=(b == 0), stop=(b == HP - 1),
                )
            return acc

        nc.vector.memset(w4_sc_raw[:].bitcast(I32), 0)
        nc.vector.memset(v_sc_all[:].bitcast(I32), 0)
        nc.gpsimd.memset(v2_sc_all[:].bitcast(I32), 0)
        nc.gpsimd.memset(v3_sc_all[:].bitcast(I32), 0)
        load_stacked(v3_sc_all, tab3_scales)
        load_stacked(v2_sc_all, tab2_scales)

        nc.sync.dma_start(lists[0][:], offs)
        nc.sync.dma_start(
            out=w4_raw[:].bitcast(I32).rearrange("p (a n) -> p a n", a=KP), in_=w4_words.bitcast(I32).rearrange("a p n -> p a n")
        )
        load_side_by_side(w4_sc_raw, w4_scales)
        w1_raw = {(0, 0): load_w1(0, 0)}
        v_all = [load_words("v", tab_words, 0)]
        load_side_by_side(v_sc_all, tab_scales)
        w1_raw[0, 1] = load_w1(0, 1)
        v_all.append(load_words("v", tab_words, 1))
        nc.sync.dma_start(out=bias[:], in_=b1.rearrange("(b p t) -> p b t", p=P, t=PACK))
        nc.sync.dma_start(out=gains[:], in_=gain.rearrange("(b p t) -> p b t", p=P, t=PACK))
        w1_raw[0, 2] = load_w1(0, 2)
        v_all.append(load_words("v", tab_words, 2))
        nc.sync.dma_start(lists[1][:], offs2)
        nc.sync.dma_start(lists[2][:], offs3)
        w1_raw[1, 0] = load_w1(1, 0)
        res_sb = [load_res(0)]
        w1_raw[1, 1] = load_w1(1, 1)

        for a in range(KP):
            cols = slice(a * H, (a + 1) * H)
            nc.vector.tensor_copy(
                out=w4_dealt[:, cols].rearrange("p (b t c i) -> p b c t i", b=HP, t=PACK, i=8),
                in_=w4_raw[:, cols].rearrange("p (b c i t) -> p b c t i", b=HP, t=PACK, i=8),
            )
        nc.vector.tensor_copy(
            out=w4_sc[:].rearrange("p (g t c i) -> p g c t i", g=KP * HP, t=PACK, i=16),
            in_=w4_sc_raw[:].rearrange("p (g c i t) -> p g c t i", g=KP * HP, t=PACK, i=16),
        )

        v, v_sc, w1q = [], [], []
        for a in range(KP):
            v.append(gather("v%d" % a, v_all[a][:], lists[0], U32))
            v_sc.append(gather("v_sc%d" % a, v_sc_all[:, a * T : (a + 1) * T], lists[0], U8))
            w1q.append(quantize_w1(0, a, w1_raw[0, a]))

        w1_raw[1, 2] = load_w1(1, 2)
        res_sb.append(load_res(1))
        v3_all = [load_words("v3", tab3_words, a) for a in range(HP)]
        v2_all = [load_words("v2", tab2_words, a) for a in range(HP)]
        fits = []
        for m in range(MT):
            fits.append(held("fit%d" % m, [P, S], F32))
            nc.sync.dma_start(out=fits[m][:], in_=fit[m * P : (m + 1) * P, :])

        hd = [donor_features(0, w1q, v, v_sc)]
        ht = [team_features(0, res_sb[0], v, v_sc)]
        w1q = [quantize_w1(1, a, w1_raw[1, a]) for a in range(KP)]
        v3_sc = gather("v3_sc", v3_sc_all[:], lists[2], U8)
        v2_sc = gather("v2_sc", v2_sc_all[:], lists[1], U8)
        hd.append(donor_features(1, w1q, v, v_sc))
        ht.append(team_features(1, res_sb[1], v, v_sc))

        v3 = [gather("v3_%d" % a, v3_all[a][:], lists[2], U32) for a in range(HP)]
        e3 = [scores(m, v3, v3_sc, ht) for m in range(MT)]
        v2 = [gather("v2_%d" % a, v2_all[a][:], lists[1], U32, pieces=1 + a) for a in range(HP)]
        for m in range(MT):
            e2 = scores(m, v2, v2_sc, hd)
            nc.vector.tensor_tensor(out=fits[m][:], in0=e2[:], in1=fits[m][:], op=ALU.mult)
            nc.vector.tensor_tensor(out=fits[m][:], in0=e3[m][:], in1=fits[m][:], op=ALU.max)
            nc.sync.dma_start(out=out[m * P : (m + 1) * P, :], in_=fits[m][:])
